import numpy as np, ml_dtypes
CORES = [9,25,41,57]
N = 4
BF = ml_dtypes.bfloat16
def gentries(a):
    return np.ascontiguousarray(a.reshape(8, 16, -1).transpose(0, 2, 1)).reshape(8, -1)
def gtable(e):
    e = np.asarray(e); return np.ascontiguousarray(e.reshape(8, -1, 16).transpose(0, 2, 1)).reshape(128, -1).astype(np.int32)
H, W, P = 128, 64, 8192
A, B, Q = 8, 64, 512
SW = 2
def pack(F, U, S, J):
    return {"fr": np.ascontiguousarray(F).reshape(N, 128, P).astype(np.float32).astype(BF), "qu": np.ascontiguousarray(U).reshape(N, 128, Q).astype(np.float32).astype(BF),
            "st": np.stack([gtable(v) for v in S]), "ju": np.stack([gtable(v) for v in J])}
def jumps(rng):
    n = (N, 8, SW * Q)
    return np.where(rng.random(n) < 0.5, rng.integers(-2, 3, n) * W + rng.integers(-2, 3, n), rng.integers(1 - P, P, n))
def scene(rng):
    base = rng.integers(0, 16, (8, 16, H, W)); dy = np.add.accumulate(rng.integers(-1, 2, (N, 8)), axis=0); dx = np.add.accumulate(rng.integers(-1, 2, (N, 8)), axis=0)
    F = np.zeros((N, 8, 16, H, W), np.int64); U = np.zeros((N, 8, 16, A, B), np.int64); S = np.zeros((N, 8, Q), np.int64)
    for r in range(N):
        for g in range(8):
            F[r, g] = np.roll(base[g], (int(dy[r, g]), int(dx[r, g])), axis=(1, 2))
            yy = (rng.integers(0, H) + np.arange(A)) % H; xx = (rng.integers(0, W) + np.arange(B)) % W
            U[r, g] = base[g][:, yy][:, :, xx]
            S[r, g] = (((yy + dy[r, g]) % H)[:, None] * W + ((xx + dx[r, g]) % W)[None, :]).reshape(-1)
    F = np.where(rng.random(F.shape) < 0.1, rng.integers(0, 16, F.shape), F); U = np.where(rng.random(U.shape) < 0.2, rng.integers(0, 16, U.shape), U)
    S = np.where(rng.random(S.shape) < 0.1, S, rng.integers(0, P, S.shape))
    return F.reshape(N, 8, 16, P), U.reshape(N, 8, 16, Q), S, jumps(rng)
def setup_inputs(rng):
    return pack(*scene(rng))
def setup_inputs_ties(rng):
    pat = rng.integers(0, 16, (8, 13, 16)); g = np.arange(8)[None, :, None]
    sub = np.argsort(rng.random((N, 8, 12)), axis=-1)[..., :6]
    idx = np.take_along_axis(sub, rng.integers(0, 6, (N, 8, P)), axis=-1)
    F = pat[g, idx].transpose(0, 1, 3, 2); U = pat[g, rng.integers(0, 13, (N, 8, Q))].transpose(0, 1, 3, 2)
    return pack(F, U, rng.integers(0, P, (N, 8, Q)), jumps(rng))
def setup_inputs_edges(rng):
    F, U, S, J = scene(rng)
    S = rng.choice(np.array([0, 1, H - 2, H - 1]), S.shape) * W + rng.choice(np.array([0, 1, W - 2, W - 1]), S.shape)
    J = rng.choice(np.array([0, 1, -1, W, -W, W - 1, P - 1, 1 - P]), J.shape)
    return pack(F, U, S, J)
def setup_inputs_far(rng):
    F = 15 * rng.integers(0, 2, (N, 8, 16, P)); U = 15 * rng.integers(0, 2, (N, 8, 16, Q)); h = rng.integers(0, 8)
    F[:, h] = 15; U[:, h] = 0
    return pack(F, U, rng.integers(0, P, (N, 8, Q)), jumps(rng))
def setup_inputs_one(rng):
    F, U, S, J = scene(rng)
    S = np.zeros_like(S) + rng.integers(0, P, (N, 8, 1)); J = np.zeros_like(J) + rng.integers(1 - P, P, (N, 8, 1))
    J[rng.integers(0, N)] = 0; k = rng.integers(0, N); F[k] = F[k][:, :, :1]
    return pack(F, U, S, J)
def setup_inputs_spread(rng):
    def uneven(n):
        e = np.exp2(rng.integers(-2, 4, (N, 8, 1, n))); v = np.minimum(np.floor(16 * rng.random((N, 8, 16, n)) ** e), 15)
        return v * (rng.random((N, 8, 1, n)) > 0.0625)
    F = uneven(P); U = uneven(Q)
    S = np.minimum(np.floor(P * rng.random((N, 8, Q)) ** 3), P - 1).astype(np.int64); S[:, :, 5] = P - 1
    J = rng.integers(1 - P, P, (N, 8, SW * Q)); J[:, :, 0] = P - 1; J[:, :, 1] = 1 - P
    return pack(F, U, S, J)
def check_inputs(d):
    bad = []
    for nm in ("fr", "qu"):
        v = d[nm].astype(np.float32)
        if not (np.isfinite(v).all() and (v == np.floor(v)).all() and v.min() >= 0 and v.max() <= 15): bad.append(nm)
    if d["st"].min() < 0 or d["st"].max() > P - 1: bad.append("st")
    if d["ju"].min() < 1 - P or d["ju"].max() > P - 1: bad.append("ju")
    return bad
def sides(p, t):
    i = np.arange(Q)
    if t == 1:
        a = np.roll(p, -1, axis=1); b = np.roll(p, -B, axis=1)
        return np.where(i % B < B - 1, a - (a % W > 0), p), np.where(i < Q - B, np.where(b >= W, b - W, b), p)
    a = np.roll(p, 1, axis=1); b = np.roll(p, B, axis=1)
    return np.where(i % B > 0, a + (a % W < W - 1), p), np.where(i >= B, np.where(b + W < P, b + W, b), p)
def reference(fr, qu, st, ju):
    F = fr.astype(np.int32).reshape(N, 8, 16, P); U = qu.astype(np.int32).reshape(N, 8, 16, Q)
    yc = np.zeros((N, 128, Q // 16), np.float32); yf = np.zeros_like(yc); yp = np.zeros_like(yc)
    for r in range(N):
        p = gentries(st[r]).astype(np.int64)
        bc = np.full((8, Q), 1 << 20, np.int64); bf = np.zeros((8, Q), np.int64); bp = np.zeros((8, Q), np.int64)
        for s in range(N):
            k = (r + s) % N; J = gentries(ju[k]).astype(np.int64).reshape(8, SW, Q)
            for t in range(SW):
                one, two = sides(p, t)
                c = np.stack([p, one, two, np.minimum(np.maximum(p + J[:, t], 0), P - 1)], axis=1)
                v = np.take_along_axis(F[k], c.reshape(8, 1, 4 * Q), axis=2).reshape(8, 16, 4, Q) - U[r][:, :, None, :]
                e = np.sum(v * v, axis=1); w = np.argmin(e, axis=1)[:, None]
                p = np.take_along_axis(c, w, axis=1)[:, 0]; best = np.take_along_axis(e, w, axis=1)[:, 0]
            m = best < bc
            bc = np.where(m, best, bc); bf = np.where(m, k, bf); bp = np.where(m, p, bp)
        yc[r] = gtable(bc); yf[r] = gtable(bf); yp[r] = gtable(bp)
    return {"yc": yc, "yf": yf, "yp": yp}

@@ -1,0 +1,506 @@
+import math
+import numpy as np
+from concourse.bass import DstId, RemoteDMATransfer
+from concourse.mybir import AluOpType as A, ActivationFunctionType as AF
+
+N = 4
+CUTS = [[0, 3, 8], [0, 4, 8], [0, 4, 8], [0, 5, 8]]
+SGATHER = [(0, 0), (0, 2), (1, 2), (1, 3)]
+NSTR = len(CUTS[0]) - 1
+ND = 2
+KS = 16384.0
+BIG = KS * 8192
+NS = (4, 6)
+POS = ((0, 1, 2, 3), (1, 0, 2, 4, 5, 3))
+FRAC = ((0, 1, 2, 3), (0, 4, 5, 6))
+LW = 108
+
+SCRATCH = {
+    "F": ("sbuf", [128, 8320], "bfloat16"),
+    "Q": ("sbuf", [128, 2048], "bfloat16"),
+    "Q2": ("sbuf", [128, 128], "float32"),
+    "STI": ("sbuf", [128, 32], "int32"),
+    "JUI": ("sbuf", [128, 64], "int32"),
+    "JF": ("sbuf", [128, 64], "float32"),
+    "LAND": ("sbuf", [128, 4 * LW], "float32"),
+    "MSG": ("sbuf", [128, 3 * LW], "float32"),
+    "FMSG": ("sbuf", [128, 96], "float32"),
+    "FLAND": ("sbuf", [128, 96], "float32"),
+    "AI": ("sbuf", [128, 64], "int32"),
+    "L0": ("sbuf", [128, 8 * 36], "uint16"),
+    "L1": ("sbuf", [128, 8 * 32], "uint16"),
+    "L3": ("sbuf", [128, 8 * 32], "uint16"),
+    "S3": ("sbuf", [128, 8 * 32], "float32"),
+    "LT": ("sbuf", [128, 8 * 32], "float32"),
+    "YR": ("sbuf", [128, 8 * 3 * 34], "bfloat16"),
+    "FL": ("sbuf", [128, 8 * 3 * 34], "bfloat16"),
+    "PA": ("sbuf", [128, 8 * 192], "float32"),
+    "MM": ("sbuf", [128, 8 * 192], "float32"),
+    "BV": ("sbuf", [128, 2 * 192], "float32"),
+    "SC": ("sbuf", [128, 8 * 192], "float32"),
+    "KI": ("sbuf", [128, 8 * 192], "float32"),
+    "RST": ("sbuf", [128, 2 * 192], "float32"),
+    "SQ0": ("sbuf", [128, 128, 16], "bfloat16"),
+    "SQ1": ("sbuf", [128, 96, 16], "bfloat16"),
+    "DF": ("sbuf", [128, 8 * 512], "bfloat16"),
+    "QSQ": ("sbuf", [128, 512], "bfloat16"),
+    "W": ("sbuf", [128, 2048], "bfloat16"),
+    "EB": ("sbuf", [128, 8], "bfloat16"),
+    "DD": ("sbuf", [128, 128], "float32"),
+    "CF": ("sbuf", [128, 5 * 128], "float32"),
+    "CB": ("sbuf", [128, 6 * 128], "bfloat16"),
+    "PI": ("sbuf", [128, 4], "int32"),
+    "MK": ("sbuf", [128, 4], "float32"),
+}
+for _x in range(NSTR):
+    SCRATCH["KA%d" % _x] = ("psum", [128, 512], "float32")
+    SCRATCH["KB%d" % _x] = ("psum", [128, 512], "float32")
+    for _d in range(ND):
+        SCRATCH["DP%d_%d" % (_x, _d)] = ("psum", [128, 512], "float32")
+
+SEMAPHORES = (["cV", "cS", "cP", "cG", "left", "sq", "lf", "lg", "lst", "lq", "lj", "lpa", "lpb"]
+              + ["q%d" % j for j in (1, 2, 3)]
+              + ["a%d_%d" % (s, x) for s in (1, 2, 3, 4) for x in range(NSTR)]
+              + ["o%d_%d" % (x, k) for x in range(NSTR) for k in range(3)])
+
+PARS = ((1.0, 1.56, 0.55, 110.0, 2600.0, 700.0), (0.9, 1.1, 0.45, 60.0, 2000.0, 500.0), (1.2, 2.0, 0.9, 160.0, 3600.0, 900.0))
+LOAD, ROUNDS = 7000.0, 30000
+_MASKS, _ORDER = {}, []
+
+
+def _mask(name, idx):
+    key = (name, repr(idx))
+    if key not in _MASKS:
+        z = np.zeros(SCRATCH[name][1][1:], np.uint8)
+        z[idx] = 1
+        _MASKS[key] = (int.from_bytes(np.packbits(z.reshape(-1), bitorder="little").tobytes(), "little"), int(z.sum()))
+    return _MASKS[key]
+
+
+def build(g, core, T, topo, par):
+    CYC, GAM, PEC, LAT, HOP, ISSUE = par
+    rank = T.rank_of(core)
+    ops, acc, bank = [], {}, {}
+
+    def R(name, *idx):
+        m, n = _mask(name, idx)
+        return (T[name][(slice(None),) + idx], name, m, n)
+
+    def C(name, a, b, st=None):
+        return R(name, slice(a, b, st))
+
+    def add(eng, emit, reads, writes, dur, sem=None, cnt=1, after=(), order=(), lat=None, hold=None):
+        k = len(ops)
+        deps, soft = set(after), set(order)
+        for refs, wr in ((reads, False), (writes, True)):
+            for r in refs:
+                name, m = r[1], r[2]
+                lst = acc.setdefault(name, [])
+                for (j, w, mj) in lst:
+                    if j != k and (w or wr) and (m & mj):
+                        psum_pe = eng == "P" and ops[j]["eng"] == "P"
+                        (soft if psum_pe else deps).add(j)
+                if wr:
+                    lst[:] = [e for e in lst if e[2] & ~m]
+                lst.append((k, wr, m))
+                if SCRATCH[name][0] == "psum":
+                    b = bank.setdefault(name, [eng, [], []])
+                    if b[0] != eng:
+                        b[0], b[2], b[1] = eng, b[1], []
+                    deps.update(b[2])
+                    b[1].append(k)
+        ops.append(dict(eng=eng, emit=emit, deps=deps, soft=soft - deps, dur=dur, sem=sem, cnt=cnt,
+                        lat=LAT if lat is None else lat, hold=dur if hold is None else hold))
+        return k
+
+    def vdur(n, f=1.0):
+        return max(64, n * f) * CYC
+
+    def ts(out, in0, s1, s2, op0, op1=None, extra=()):
+        if op1 is None:
+            e = lambda q: q.tensor_scalar(out[0], in0[0], s1, None, op0)
+        else:
+            e = lambda q: q.tensor_scalar(out[0], in0[0], s1, s2, op0, op1)
+        return add("V", e, [in0] + list(extra), [out], vdur(out[3]))
+
+    def tt(out, a, b, op):
+        f = 1.0 if "psum" in (SCRATCH[a[1]][0], SCRATCH[b[1]][0]) else 2.0
+        return add("V", lambda q: q.tensor_tensor(out[0], a[0], b[0], op), [a, b], [out], vdur(out[3], f))
+
+    def vcopy(out, a):
+        return add("V", lambda q: q.tensor_copy(out[0], a[0]), [a], [out], vdur(out[3]))
+
+    def mset(out, v):
+        f = 0.5 if SCRATCH[out[1]][2] in ("bfloat16", "uint16") else 1.0
+        return add("V", lambda q: q.memset(out[0], v), [], [out], vdur(out[3], f))
+
+    def scan(out, d0, d1, op0, op1):
+        return add("V", lambda q: q.tensor_tensor_scan(out[0], d0[0], d1[0], 0.0, op0, op1), [d0, d1], [out], vdur(out[3]))
+
+    def act(out, a, func, bias=None, extra=()):
+        kw = {} if bias is None else {"bias": bias}
+        return add("S", lambda q: q.activation(out[0], a[0], func, **kw), [a] + list(extra), [out], (65 + out[3]) * CYC)
+
+    def mm(out, lst, start, stop):
+        def e(q):
+            for i, (l, r) in enumerate(lst):
+                ins = q.matmul(out[0], l[0], r[0], start and i == 0, stop and i == len(lst) - 1)
+            return ins
+        d = sum(max(64, r[3]) * (4 if SCRATCH[r[1]][2] == "float32" else 1) for l, r in lst) * PEC
+        return add("P", e, [x for p in lst for x in p], [out], d)
+
+    def dma(eng, out, in_, sem, reads, writes, lat, order=()):
+        return add(eng, lambda q: q.dma_start(out, in_), reads, writes, lat, sem=sem, cnt=16, lat=0, hold=60, order=order)
+
+    sent = [0]
+
+    def send(to, src, dst, sem, lat, after=(), order=()):
+        c = T.cores[to % N]
+        rid, pid, _ = topo.addr(c)
+        ne = len(topo.engines(core, c))
+        sent[0] += ne
+        k = add("G", lambda q: q.remote_dma(dst[0], src[0], T.sem[sem], T.sem.left, pid, rid, topo.mask(core, c)),
+                [src], [], ISSUE, sem="", after=after, order=order, lat=0)
+        add(None, None, [], [dst], lat, sem=sem, cnt=ne, after=[k], lat=0)
+        return k
+
+    k = dma("Y", T.STI[:], T.st[:], "lst", [], [C("STI", 0, 32)], 2000)
+    lf = dma("Y", T.F[:, 64:4160], T.fr[:, 0:4096], "lf", [], [C("F", 64, 4160)], LOAD - 500, [k])
+    k = dma("Y", T.F[:, 0:64], T.fr[:, 0:64], "lpa", [], [C("F", 0, 64)], LOAD - 500, [lf])
+    dma("Y", T.F[:, 8256:8320], T.fr[:, 8128:8192], "lpb", [], [C("F", 8256, 8320)], LOAD - 500, [k])
+    k = dma("S", T.Q[:, 0:512], T.qu[:], "lq", [], [C("Q", 0, 512)], 2300)
+    k = dma("S", T.JUI[:], T.ju[:], "lj", [], [C("JUI", 0, 64)], 2400, [k])
+    lg = dma("S", T.F[:, 4160:8256], T.fr[:, 4096:8192], "lg", [], [C("F", 4160, 8256)], LOAD, [k])
+
+    DD = C("DD", 0, 128)
+    add("G", lambda q: q.iota(DD[0], [[1, 128]], 0, -1, allow_small_or_imprecise_dtypes=True), [], [DD], 350)
+    add("G", lambda q: q.affine_select(DD[0], DD[0], [[-16, 8], [0, 16]], A.is_ge, 999.0, 0, 1), [DD], [DD], 400)
+    add("G", lambda q: q.affine_select(DD[0], DD[0], [[16, 8], [0, 16]], A.is_ge, 999.0, 15, -1), [DD], [DD], 400)
+    PI0, PI1 = C("PI", 0, 1), C("PI", 1, 2)
+    add("G", lambda q: q.iota(PI0[0], [[0, 1]], 0, 1), [], [PI0], 140)
+    ts(PI1, PI0, 15, None, A.bitwise_and)
+    MK = (C("MK", 0, 1), C("MK", 1, 2))
+    for t in (0, 1):
+        ts(MK[t], PI1, 15.0 * t, BIG, A.is_equal, A.mult)
+        ts(MK[t], MK[t], KS * FRAC[t][1] / 64, None, A.add)
+    cf = lambda i: C("CF", 128 * i, 128 * i + 128)
+    cb = lambda i: C("CB", 128 * i, 128 * i + 128)
+    for i, v in enumerate((1.0, -15.0, -1.0, 15.0, 0.0)):
+        ts(cf(i), DD, v, None, A.is_equal)
+        ts(cb(i), DD, v, (1 / 64, 1 / 64, -1 / 64, -1 / 64, 1.0)[i], A.is_equal, A.mult)
+    ts(cb(5), DD, 0.0, -2.0, A.is_equal, A.mult)
+    mset(C("W", 0, 2048), 0.0)
+    EB = C("EB", 0, 8)
+    ts(EB, C("DD", 0, 128, 16), 999.0, KS, A.not_equal, A.mult)
+    for r in range(16):
+        act(C("W", 128 * r + r, 128 * r + 128, 16), EB, AF.Copy)
+    Wr = lambda r: C("W", 128 * r, 128 * r + 128)
+    mset(C("RST", 0, 384), 0.0)
+    for t in (0, 1):
+        ns, b = NS[t], 192 * t
+        edge = C("KI", b + POS[t][1] + (0, 3)[t] * ns, b + 32 * ns, 4 * ns)
+        for c in range(ns):
+            mset(C("KI", b + POS[t][c], b + 32 * ns, ns), KS * FRAC[t][c] / 64 if c < 4 else KS * 16000)
+        ts(edge, edge, 0.0, MK[t][0], A.mult, A.add, extra=[MK[t]])
+        mset(C("KI", b + 2 + (0, 28)[t] * ns, b + (4, 32)[t] * ns, ns), BIG + KS * FRAC[t][2] / 64)
+        mset(C("RST", b, b + 32 * ns, ns), 2.0 ** 30)
+    mset(C("LAND", 0, LW), 128.0)
+    for s in range(3):
+        mset(C("MSG", s * LW, s * LW + 12), 128.0)
+    for s in range(4):
+        mset(C("SC", 384 * s + 128, 384 * s + 144), 128.0)
+        mset(C("PA", 384 * s + 192 + POS[1][5], 384 * s + 384, NS[1]), 128.0)
+        mset(C("L0", 72 * s + 68, 72 * s + 72), 0)
+    ts(C("LAND", 12, LW, 3), C("STI", 0, 32), 1 / 64, 128.0, A.mult, A.add)
+    ts(C("JF", 0, 64), C("JUI", 0, 64), 1 / 64, None, A.mult)
+
+    act(C("QSQ", 0, 512), C("Q", 0, 512), AF.Square)
+    mm(C("KA0", 448, 480), [(Wr(r), C("QSQ", r, 512, 16)) for r in range(16)], True, True)
+    act(C("Q2", 0, 32), C("KA0", 448, 480), AF.Copy)
+
+    first = send(rank + 1, C("Q", 0, 512), C("Q", 512, 1024), "q1", 4500, after=[lf, lg])
+    peers = [T.cores[(rank + j) % N] for j in (1, 2, 3)]
+    m = topo.mask(core, peers[0]) & topo.mask(core, peers[1]) & topo.mask(core, peers[2])
+    ne = bin(m).count("1")
+    sent[0] += ne
+    tr = RemoteDMATransfer(dst_ids=[DstId(rid=topo.addr(c)[0], pnc=topo.addr(c)[1]) for c in peers], dma_engine_mask=m,
+                           remote_sem=T.sem.sq, srcs=[T.Q2[:, 0:32]], dsts=[T.Q2[:, 32 * j:32 * j + 32] for j in (1, 2, 3)])
+    k = add("G", lambda q: q.remote_dma_fused([tr], local_sem=T.sem.left), [C("Q2", 0, 32)], [], ISSUE, sem="", order=[first], lat=0)
+    add(None, None, [], [C("Q2", 32, 128)], 4000, sem="sq", cnt=3 * ne, after=[k], lat=0)
+
+    for s in range(1, N):
+        act(C("KI", 384 * s, 384 * s + 128), C("KI", 0, 128), AF.Copy)
+        act(C("KI", 384 * s + 192, 384 * s + 384), C("KI", 192, 384), AF.Copy)
+    for s in range(N):
+        for (t, c) in SGATHER:
+            ns, o = NS[t], 384 * s + 192 * t + POS[t][c]
+            a, b = ((4, 32), (0, 28))[t] if c == 2 else (0, 32)
+            act(C("KI", o + ns * a, o + ns * (b - 1) + 1, ns), C("Q2", 32 * s + a, 32 * s + b), AF.Identity, bias=KS * FRAC[t][c] / 64)
+            if c == 1:
+                a = (0, 3)[t]
+                act(C("KI", o + ns * a, o + ns * 31 + 1, 4 * ns), C("Q2", 32 * s + a, 32 * s + 32, 4), AF.Identity,
+                    bias=MK[t][0], extra=[MK[t]])
+
+    WIN = {0: 64, 1: 128, -1: 0}
+
+    def star(s, t, a, b):
+        if t == 0:
+            o = s * LW + 12
+            return C("LAND", o + 3 * a, o + 3 * (b - 1) + 1, 3)
+        o = 384 * s + 3
+        return C("SC", o + 4 * a, o + 4 * (b - 1) + 1, 4)
+
+    def lists0(s, t, a, b):
+        o = 72 * s + (4, 36)[t]
+        ts(C("L0", o + a, o + b), star(s, t, a, b), 64.0, 8192.0, A.mult, A.subtract)
+
+    def sweep(s, t, x):
+        c0, c1 = 4 * CUTS[s][x], 4 * CUTS[s][x + 1]
+        n, ns, u, sg = c1 - c0, NS[t], 2 * s + t, (1, -1)[t]
+        slot = lambda nm, c: C(nm, 192 * u + ns * c0 + POS[t][c], 192 * u + ns * c1, ns)
+        full = lambda nm, base: C(nm, base + ns * c0, base + ns * c1)
+        SQ, nq = "SQ%d" % t, 4 - t
+        kb = ("KA%d", "KB%d")[t] % x
+        K, KQ, E, P1 = C(kb, 0, ns * n), C(kb, 0, ns * n, 1 + t), C(kb, 200, 200 + ns * n), C(kb, 400, 400 + n)
+        me = star(s, t, c0, c1)
+        if t == 1:
+            lists0(s, 1, c0, c1)
+        l0 = 72 * s + (4, 36)[t]
+        a, b = (c0 - 1, c1) if t == 0 else (c0, c1 + 1)
+        fo = (u * 3 + x) * 34
+        YR, FL = C("YR", fo, fo + n + 1), C("FL", fo, fo + n + 1)
+        if t == 0:
+            act(YR, star(s, t, a, b), AF.Identity, bias=-61.0 / 128)
+            tt(FL, YR, star(s, t, a, b), A.is_le)
+            f_me, f_nb = C("FL", fo + 1, fo + n + 1), C("FL", fo, fo + n)
+        else:
+            act(YR, star(s, t, a, b), AF.Copy)
+            tt(FL, YR, star(s, t, a, b), A.not_equal)
+            f_me, f_nb = C("FL", fo, fo + n), C("FL", fo + 1, fo + n + 1)
+        mm(P1, [(cf(2 * t), me), (cf(2 * t + 1), star(s, t, c0 - sg, c1 - sg))], True, False)
+        mm(P1, [(cb(2 * t), f_me), (cb(2 * t + 1), f_nb)], False, True)
+        ts(C("L1", 32 * u + c0, 32 * u + c1), P1, 64.0, 8192.0, A.mult, A.subtract)
+        act(slot("PA", 1), P1, AF.Copy)
+        S3 = C("S3", 32 * u + c0, 32 * u + c1)
+        tt(S3, me, C("JF", 32 * t + c0, 32 * t + c1), A.add)
+        ts(slot("PA", 3), S3, 128.0, 256 - 1 / 64, A.max, A.min)
+        ts(C("L3", 32 * u + c0, 32 * u + c1), slot("PA", 3), 64.0, 8192.0, A.mult, A.subtract)
+        LT, nb = C("LT", 32 * u + c0, 32 * u + c1), star(s, t, c0 - 4 * sg, c1 - 4 * sg)
+        ts(LT, nb, (255.0, 129.0)[t], None, (A.is_lt, A.is_ge)[t])
+        tt(slot("PA", 2), nb, LT, (A.add, A.subtract)[t])
+        act(slot("PA", 0), me, AF.Copy)
+        if t == 1:
+            act(slot("KI", 0), C("MM", 384 * s + 4 * c0 + 3, 384 * s + 4 * c1, 4), AF.Copy)
+            o = s * LW + 12
+            act(slot("PA", 4), C("LAND", o + 3 * c0 + 1, o + 3 * c1, 3), AF.Copy)
+            if s > 0:
+                act(slot("KI", 4), C("LAND", o + 3 * c0 + 2, o + 3 * c1, 3), AF.Copy)
+        offs = {0: ("L0", l0), 1: ("L1", 32 * u), 2: ("L0", l0 - 4 * sg), 3: ("L3", 32 * u)}
+        qq = C("Q", 512 * s + 16 * c0, 512 * s + 16 * c1)
+        nd = 0
+        for c in ((0, 2, 3, 1) if t == 0 else (2, 3, 1)):
+            w0 = WIN[sg if c == 2 else 0]
+            win = C("F", w0, w0 + 8192)
+            of = C(offs[c][0], offs[c][1] + c0, offs[c][1] + c1)
+            df = C("DF", 512 * (4 * t + c) + 16 * c0, 512 * (4 * t + c) + 16 * c1)
+            sq = R(SQ, slice(nq * c0 + c - t, nq * c1, nq), slice(None))
+            if (t, c) in SGATHER:
+                D = C("DP%d_%d" % (x, nd % ND), 0, 16 * n)
+                nd += 1
+                mm(D, [(cb(5), qq)], True, False)
+                add("S", lambda q, df=df, win=win, of=of: q.activation(df[0], win[0].indirect(of[0]), AF.Copy),
+                    [win, of], [df], (65 + df[3] * GAM) * CYC)
+                mm(D, [(cb(4), df)], False, True)
+                tt(sq, D, df, A.mult)
+            else:
+                add("V", lambda q, df=df, win=win, of=of: q.tensor_tensor(df[0], win[0].indirect(of[0]), qq[0], A.subtract),
+                    [win, of, qq], [df], (50 + df[3] * GAM) * CYC)
+                act(sq, df, AF.Square)
+        mm(K, [(cf(4), full("KI", 192 * u))], True, False)
+        mm(KQ, [(Wr(r), R(SQ, slice(nq * c0, nq * c1), r)) for r in range(16)], False, True)
+        M = full("MM", 192 * u)
+        scan(M, C("RST", 192 * t, 192 * t + ns * n), K, A.add, A.min)
+        tt(E, K, M, A.subtract)
+        tt(full("BV", 192 * t), full("PA", 192 * u), E, A.subtract)
+        scan(full("SC", 192 * u), E, full("BV", 192 * t), A.min, A.max)
+        if t == 0:
+            return None
+        if s < 3:
+            o = s * LW + 12
+            act(C("MSG", o + 3 * c0 + 2, o + 3 * c1, 3), slot("MM", 4), AF.Identity, bias=-KS / 4)
+            vcopy(C("MSG", o + 3 * c0, o + 3 * c1, 3), slot("SC", 3))
+            act(C("MSG", o + 3 * c0 + 1, o + 3 * c1, 3), slot("SC", 4), AF.Copy)
+            a = c0 if c0 else -4
+            k = send(rank + 1, C("MSG", o + 3 * a, o + 3 * c1), C("LAND", o + LW + 3 * a, o + LW + 3 * c1), "a%d_%d" % (s + 1, x), HOP)
+            lists0(s + 1, 0, a, c1)
+            return k
+        owner = (rank + 1) % N
+        best = slot("MM", 4)
+        ci, fi = C("AI", 2 * c0, 2 * c0 + n), C("AI", 2 * c0 + n, 2 * c1)
+        ts(ci, best, 1 / KS, 0.33, A.mult, A.add)
+        ts(fi, best, 4 / KS, owner + 3 - 0.19, A.mult, A.add)
+        ts(fi, fi, 3, None, A.bitwise_and)
+        vcopy(C("FMSG", 3 * c0 + n, 3 * c1), C("AI", 2 * c0, 2 * c1))
+        ts(C("FMSG", 3 * c0, 3 * c0 + n), slot("SC", 4), 128.0, 64.0, A.subtract, A.mult)
+        k = send(rank + 1, C("FMSG", 3 * c0, 3 * c1), C("FLAND", 3 * c0, 3 * c1), "a4_%d" % x, HOP)
+        for j, y in enumerate((T.yp, T.yc, T.yf)):
+            src = C("FLAND", 3 * c0 + j * n, 3 * c0 + (j + 1) * n)
+            dma("S" if (x == 0 and j == 1) else "Y", y[:, c0:c1], src[0], "o%d_%d" % (x, j), [src], [], 2000)
+        return k
+
+    lists0(0, 0, -4, 32)
+    for s in range(N):
+        xs = list(range(NSTR - 1, -1, -1))
+        for x in xs:
+            sweep(s, 0, x)
+        for x in xs:
+            last = sweep(s, 1, x)
+        if s < 2:
+            send(rank + s + 2, C("Q", 0, 512), C("Q", 512 * (s + 2), 512 * (s + 3)), "q%d" % (s + 2), 4000, order=[last])
+    return ops, sent[0]
+
+
+def links(ops):
+    return [[(j, ops[j]["dur"] + ops[j]["lat"]) for j in sorted(o["deps"])] + [(j, ops[j]["hold"]) for j in sorted(o["soft"])] for o in ops]
+
+
+def schedule(ops):
+    n, pre = len(ops), links(ops)
+    succ = [[] for _ in ops]
+    for k in range(n):
+        for j, d in pre[k]:
+            succ[j].append((k, d))
+    prio = [0.0] * n
+    for k in range(n - 1, -1, -1):
+        prio[k] = ops[k]["dur"] + ops[k]["lat"] + max([prio[j] for j, _ in succ[k]] or [0.0])
+    left, ready, free, order = [len(p) for p in pre], [0.0] * n, {}, []
+    avail = [k for k in range(n) if left[k] == 0]
+    while avail:
+        k = min(avail, key=lambda k: (max(ready[k], free.get(ops[k]["eng"], 0.0)), -prio[k], k))
+        avail.remove(k)
+        st = max(ready[k], free.get(ops[k]["eng"], 0.0))
+        if ops[k]["eng"]:
+            free[ops[k]["eng"]] = st + ops[k]["hold"]
+        order.append(k)
+        for j, d in succ[k]:
+            ready[j] = max(ready[j], st + d)
+            left[j] -= 1
+            if left[j] == 0:
+                avail.append(j)
+    return order
+
+
+def replay(p, order):
+    eng, dur, hold, pre = p
+    free, last, st, why, end, ek = {}, {}, [0.0] * len(eng), [None] * len(eng), 0.0, 0
+    for k in order:
+        e = eng[k]
+        t, w = free.get(e, 0.0), (last.get(e), 1)
+        for j, d in pre[k]:
+            if st[j] + d > t:
+                t, w = st[j] + d, (j, 0)
+        st[k], why[k] = t, w
+        if e:
+            free[e], last[e] = t + hold[k], k
+        if t + dur[k] > end:
+            end, ek = t + dur[k], k
+    return end, ek, why
+
+
+def improve(sets, order):
+    ps = [([o["eng"] for o in s], [o["dur"] for o in s], [o["hold"] for o in s], links(s)) for s in sets]
+    eng, pre = ps[0][0], ps[0][3]
+    seed = [12345]
+
+    def rnd():
+        seed[0] = (seed[0] * 6364136223846793005 + 1442695040888963407) % (1 << 64)
+        return (seed[0] >> 11) / float(1 << 53)
+
+    res = [replay(p, order) for p in ps]
+    unit = [r[0] for r in res]
+    cur = float(len(ps))
+    best = (cur, order)
+    for it in range(ROUNDS):
+        r = res[int(rnd() * len(res))]
+        k, q = r[1], []
+        while k is not None:
+            j, queued = r[2][k]
+            if queued and j is not None:
+                q.append((j, k))
+            k = j
+        b, k = q[int(rnd() * len(q))]
+        pos = {v: i for i, v in enumerate(order)}
+        i = pos[b]
+        for _ in range(int(rnd() * 4) if rnd() < 0.5 else 0):
+            i -= 1
+            while i >= 0 and eng[order[i]] != eng[k]:
+                i -= 1
+            if i >= 0:
+                b = order[i]
+        anc, stack = {k}, [k]
+        while stack:
+            for j, _ in pre[stack.pop()]:
+                if pos[j] >= pos[b] and j not in anc:
+                    anc.add(j)
+                    stack.append(j)
+        if b in anc:
+            continue
+        seg = order[pos[b]:pos[k] + 1]
+        new = order[:pos[b]] + [v for v in seg if v in anc] + [v for v in seg if v not in anc] + order[pos[k] + 1:]
+        res2 = [replay(p, new) for p in ps]
+        c = sum(x[0] / w for x, w in zip(res2, unit))
+        if c <= cur or rnd() < math.exp((cur - c) / (0.004 * (1 - it / ROUNDS) + 1e-5)):
+            cur, res, order = c, res2, new
+            if c < best[0]:
+                best = (c, new)
+    return best[1]
+
+
+def rank_program(g, core, T, topo):
+    if T.rank_of(core) is None:
+        return
+    ops, sent = build(g, core, T, topo, PARS[0])
+    if not _ORDER:
+        _ORDER.extend(improve([build(g, core, T, topo, p)[0] for p in PARS], schedule(ops)))
+    order = _ORDER
+    place = {k: i for i, k in enumerate(order)}
+    queue = {"V": g.vector, "S": g.scalar, "P": g.tensor, "G": g, "Y": g.sync}
+    count = {e: 0 for e in "VSPG"}
+    known = {e: {} for e in queue}
+    token, clock = {}, {}
+    for k in order:
+        o = ops[k]
+        e = o["eng"]
+        if e is None:
+            token[k], clock[k] = (o["sem"], o["cnt"]), {}
+            continue
+        kn, need = known[e], {}
+        for j in o["deps"]:
+            sem, val = token[j]
+            need[sem] = max(need.get(sem, (0, 0)), (val, j))
+        for sem, (val, j) in sorted(need.items(), key=lambda it: -place[it[1][1]]):
+            if kn.get(sem, 0) >= val:
+                continue
+            queue[e].wait_ge(T.sem[sem], val)
+            kn[sem] = val
+            for s2, v2 in clock[j].items():
+                kn[s2] = max(kn.get(s2, 0), v2)
+        ins = o["emit"](queue[e])
+        clock[k] = dict(kn)
+        if o["sem"] is None:
+            count[e] += 1
+            ins.then_inc(T.sem["c" + e], 1)
+            token[k] = ("c" + e, count[e])
+        elif o["sem"]:
+            ins.then_inc(T.sem[o["sem"]], 16)
+            token[k] = (o["sem"], 16)
+    top = {"left": sent}
+    for sem, val in token.values():
+        top[sem] = max(top.get(sem, 0), val)
+    anyq = {}
+    for kn in known.values():
+        for sem, val in kn.items():
+            anyq[sem] = max(anyq.get(sem, 0), val)
+    for sem, val in top.items():
+        if anyq.get(sem, 0) < val:
+            g.wait_ge(T.sem[sem], val)

@@ -4,7 +4,7 @@ from concourse.bass import DstId, RemoteDMATransfer
 from concourse.mybir import AluOpType as A, ActivationFunctionType as AF
 
 N = 4
-CUTS = [[0, 3, 8], [0, 4, 8], [0, 4, 8], [0, 5, 8]]
+CUTS = [[0, 3, 8], [0, 4, 8], [0, 4, 8], [0, 4, 8]]
 SGATHER = [(0, 0), (0, 2), (1, 2), (1, 3)]
 NSTR = len(CUTS[0]) - 1
 ND = 2
@@ -58,13 +58,13 @@ for _x in range(NSTR):
     for _d in range(ND):
         SCRATCH["DP%d_%d" % (_x, _d)] = ("psum", [128, 512], "float32")
 
-SEMAPHORES = (["cV", "cS", "cP", "cG", "left", "sq", "lf", "lg", "lst", "lq", "lj", "lpa", "lpb"]
+SEMAPHORES = (["cV", "cS", "cP", "cG", "left", "sq", "lf", "lg", "lst", "lq", "lj"]
               + ["q%d" % j for j in (1, 2, 3)]
               + ["a%d_%d" % (s, x) for s in (1, 2, 3, 4) for x in range(NSTR)]
               + ["o%d_%d" % (x, k) for x in range(NSTR) for k in range(3)])
 
-PARS = ((1.0, 1.56, 0.55, 110.0, 2600.0, 700.0), (0.9, 1.1, 0.45, 60.0, 2000.0, 500.0), (1.2, 2.0, 0.9, 160.0, 3600.0, 900.0))
-LOAD, ROUNDS = 7000.0, 30000
+PARS = ((0.83, 1.1, 0.42, 120.0, 3000.0, 800.0), (1.1, 1.7, 0.55, 130.0, 3300.0, 900.0), (0.95, 1.4, 0.5, 190.0, 2400.0, 600.0))
+LOAD, ROUNDS = 9000.0, 25000
 _MASKS, _ORDER = {}, []
 
 
@@ -165,12 +165,12 @@ def build(g, core, T, topo, par):
         return k
 
     k = dma("Y", T.STI[:], T.st[:], "lst", [], [C("STI", 0, 32)], 2000)
-    lf = dma("Y", T.F[:, 64:4160], T.fr[:, 0:4096], "lf", [], [C("F", 64, 4160)], LOAD - 500, [k])
-    k = dma("Y", T.F[:, 0:64], T.fr[:, 0:64], "lpa", [], [C("F", 0, 64)], LOAD - 500, [lf])
-    dma("Y", T.F[:, 8256:8320], T.fr[:, 8128:8192], "lpb", [], [C("F", 8256, 8320)], LOAD - 500, [k])
+    lf = dma("Y", T.F[:, 64:4160], T.fr[:, 0:4096], "lf", [], [C("F", 64, 4160)], LOAD - 200, [k])
     k = dma("S", T.Q[:, 0:512], T.qu[:], "lq", [], [C("Q", 0, 512)], 2300)
-    k = dma("S", T.JUI[:], T.ju[:], "lj", [], [C("JUI", 0, 64)], 2400, [k])
     lg = dma("S", T.F[:, 4160:8256], T.fr[:, 4096:8192], "lg", [], [C("F", 4160, 8256)], LOAD, [k])
+    dma("S", T.JUI[:], T.ju[:], "lj", [], [C("JUI", 0, 64)], LOAD + 400, [lg])
+    vcopy(C("F", 0, 64), C("F", 64, 128))
+    vcopy(C("F", 8256, 8320), C("F", 8192, 8256))
 
     DD = C("DD", 0, 128)
     add("G", lambda q: q.iota(DD[0], [[1, 128]], 0, -1, allow_small_or_imprecise_dtypes=True), [], [DD], 350)
@@ -212,7 +212,7 @@ def build(g, core, T, topo, par):
         mset(C("PA", 384 * s + 192 + POS[1][5], 384 * s + 384, NS[1]), 128.0)
         mset(C("L0", 72 * s + 68, 72 * s + 72), 0)
     ts(C("LAND", 12, LW, 3), C("STI", 0, 32), 1 / 64, 128.0, A.mult, A.add)
-    ts(C("JF", 0, 64), C("JUI", 0, 64), 1 / 64, None, A.mult)
+    ts(C("JF", 0, 64), C("JUI", 0, 64), 1 / 64, 128.0, A.mult, A.subtract)
 
     act(C("QSQ", 0, 512), C("Q", 0, 512), AF.Square)
     mm(C("KA0", 448, 480), [(Wr(r), C("QSQ", r, 512, 16)) for r in range(16)], True, True)
@@ -281,10 +281,10 @@ def build(g, core, T, topo, par):
         mm(P1, [(cb(2 * t), f_me), (cb(2 * t + 1), f_nb)], False, True)
         ts(C("L1", 32 * u + c0, 32 * u + c1), P1, 64.0, 8192.0, A.mult, A.subtract)
         act(slot("PA", 1), P1, AF.Copy)
-        S3 = C("S3", 32 * u + c0, 32 * u + c1)
+        S3, L3 = C("S3", 32 * u + c0, 32 * u + c1), C("L3", 32 * u + c0, 32 * u + c1)
         tt(S3, me, C("JF", 32 * t + c0, 32 * t + c1), A.add)
-        ts(slot("PA", 3), S3, 128.0, 256 - 1 / 64, A.max, A.min)
-        ts(C("L3", 32 * u + c0, 32 * u + c1), slot("PA", 3), 64.0, 8192.0, A.mult, A.subtract)
+        ts(L3, S3, 128 - 1 / 64, 64.0, A.min, A.mult)
+        ts(slot("PA", 3), L3, 1 / 64, 128.0, A.mult, A.add)
         LT, nb = C("LT", 32 * u + c0, 32 * u + c1), star(s, t, c0 - 4 * sg, c1 - 4 * sg)
         ts(LT, nb, (255.0, 129.0)[t], None, (A.is_lt, A.is_ge)[t])
         tt(slot("PA", 2), nb, LT, (A.add, A.subtract)[t])
@@ -449,7 +449,7 @@ def improve(sets, order):
         new = order[:pos[b]] + [v for v in seg if v in anc] + [v for v in seg if v not in anc] + order[pos[k] + 1:]
         res2 = [replay(p, new) for p in ps]
         c = sum(x[0] / w for x, w in zip(res2, unit))
-        if c <= cur or rnd() < math.exp((cur - c) / (0.004 * (1 - it / ROUNDS) + 1e-5)):
+        if c <= cur or rnd() < math.exp((cur - c) / (0.003 * (1 - it / ROUNDS) + 1e-5)):
             cur, res, order = c, res2, new
             if c < best[0]:
                 best = (c, new)

import math
import numpy as np
from concourse.bass import DstId, RemoteDMATransfer
from concourse.mybir import AluOpType as A, ActivationFunctionType as AF

N = 4
CUTS = [[0, 3, 8], [0, 4, 8], [0, 4, 8], [0, 4, 8]]
SGATHER = [(0, 0), (0, 2), (1, 2), (1, 3)]
NSTR = len(CUTS[0]) - 1
ND = 2
KS = 16384.0
BIG = KS * 8192
NS = (4, 6)
POS = ((0, 1, 2, 3), (1, 0, 2, 4, 5, 3))
FRAC = ((0, 1, 2, 3), (0, 4, 5, 6))
LW = 108

SCRATCH = {
    "F": ("sbuf", [128, 8320], "bfloat16"),
    "Q": ("sbuf", [128, 2048], "bfloat16"),
    "Q2": ("sbuf", [128, 128], "float32"),
    "STI": ("sbuf", [128, 32], "int32"),
    "JUI": ("sbuf", [128, 64], "int32"),
    "JF": ("sbuf", [128, 64], "float32"),
    "LAND": ("sbuf", [128, 4 * LW], "float32"),
    "MSG": ("sbuf", [128, 3 * LW], "float32"),
    "FMSG": ("sbuf", [128, 96], "float32"),
    "FLAND": ("sbuf", [128, 96], "float32"),
    "AI": ("sbuf", [128, 64], "int32"),
    "L0": ("sbuf", [128, 8 * 36], "uint16"),
    "L1": ("sbuf", [128, 8 * 32], "uint16"),
    "L3": ("sbuf", [128, 8 * 32], "uint16"),
    "S3": ("sbuf", [128, 8 * 32], "float32"),
    "LT": ("sbuf", [128, 8 * 32], "float32"),
    "YR": ("sbuf", [128, 8 * 3 * 34], "bfloat16"),
    "FL": ("sbuf", [128, 8 * 3 * 34], "bfloat16"),
    "PA": ("sbuf", [128, 8 * 192], "float32"),
    "MM": ("sbuf", [128, 8 * 192], "float32"),
    "BV": ("sbuf", [128, 2 * 192], "float32"),
    "SC": ("sbuf", [128, 8 * 192], "float32"),
    "KI": ("sbuf", [128, 8 * 192], "float32"),
    "RST": ("sbuf", [128, 2 * 192], "float32"),
    "SQ0": ("sbuf", [128, 128, 16], "bfloat16"),
    "SQ1": ("sbuf", [128, 96, 16], "bfloat16"),
    "DF": ("sbuf", [128, 8 * 512], "bfloat16"),
    "QSQ": ("sbuf", [128, 512], "bfloat16"),
    "W": ("sbuf", [128, 2048], "bfloat16"),
    "EB": ("sbuf", [128, 8], "bfloat16"),
    "DD": ("sbuf", [128, 128], "float32"),
    "CF": ("sbuf", [128, 5 * 128], "float32"),
    "CB": ("sbuf", [128, 6 * 128], "bfloat16"),
    "PI": ("sbuf", [128, 4], "int32"),
    "MK": ("sbuf", [128, 4], "float32"),
}
for _x in range(NSTR):
    SCRATCH["KA%d" % _x] = ("psum", [128, 512], "float32")
    SCRATCH["KB%d" % _x] = ("psum", [128, 512], "float32")
    for _d in range(ND):
        SCRATCH["DP%d_%d" % (_x, _d)] = ("psum", [128, 512], "float32")

SEMAPHORES = (["cV", "cS", "cP", "cG", "left", "sq", "lf", "lg", "lst", "lq", "lj"]
              + ["q%d" % j for j in (1, 2, 3)]
              + ["a%d_%d" % (s, x) for s in (1, 2, 3, 4) for x in range(NSTR)]
              + ["o%d_%d" % (x, k) for x in range(NSTR) for k in range(3)])

PARS = ((0.83, 1.1, 0.42, 120.0, 3000.0, 800.0), (1.1, 1.7, 0.55, 130.0, 3300.0, 900.0), (0.95, 1.4, 0.5, 190.0, 2400.0, 600.0))
LOAD, ROUNDS = 9000.0, 25000
_MASKS, _ORDER = {}, []


def _mask(name, idx):
    key = (name, repr(idx))
    if key not in _MASKS:
        z = np.zeros(SCRATCH[name][1][1:], np.uint8)
        z[idx] = 1
        _MASKS[key] = (int.from_bytes(np.packbits(z.reshape(-1), bitorder="little").tobytes(), "little"), int(z.sum()))
    return _MASKS[key]


def build(g, core, T, topo, par):
    CYC, GAM, PEC, LAT, HOP, ISSUE = par
    rank = T.rank_of(core)
    ops, acc, bank = [], {}, {}

    def R(name, *idx):
        m, n = _mask(name, idx)
        return (T[name][(slice(None),) + idx], name, m, n)

    def C(name, a, b, st=None):
        return R(name, slice(a, b, st))

    def add(eng, emit, reads, writes, dur, sem=None, cnt=1, after=(), order=(), lat=None, hold=None):
        k = len(ops)
        deps, soft = set(after), set(order)
        for refs, wr in ((reads, False), (writes, True)):
            for r in refs:
                name, m = r[1], r[2]
                lst = acc.setdefault(name, [])
                for (j, w, mj) in lst:
                    if j != k and (w or wr) and (m & mj):
                        psum_pe = eng == "P" and ops[j]["eng"] == "P"
                        (soft if psum_pe else deps).add(j)
                if wr:
                    lst[:] = [e for e in lst if e[2] & ~m]
                lst.append((k, wr, m))
                if SCRATCH[name][0] == "psum":
                    b = bank.setdefault(name, [eng, [], []])
                    if b[0] != eng:
                        b[0], b[2], b[1] = eng, b[1], []
                    deps.update(b[2])
                    b[1].append(k)
        ops.append(dict(eng=eng, emit=emit, deps=deps, soft=soft - deps, dur=dur, sem=sem, cnt=cnt,
                        lat=LAT if lat is None else lat, hold=dur if hold is None else hold))
        return k

    def vdur(n, f=1.0):
        return max(64, n * f) * CYC

    def ts(out, in0, s1, s2, op0, op1=None, extra=()):
        if op1 is None:
            e = lambda q: q.tensor_scalar(out[0], in0[0], s1, None, op0)
        else:
            e = lambda q: q.tensor_scalar(out[0], in0[0], s1, s2, op0, op1)
        return add("V", e, [in0] + list(extra), [out], vdur(out[3]))

    def tt(out, a, b, op):
        f = 1.0 if "psum" in (SCRATCH[a[1]][0], SCRATCH[b[1]][0]) else 2.0
        return add("V", lambda q: q.tensor_tensor(out[0], a[0], b[0], op), [a, b], [out], vdur(out[3], f))

    def vcopy(out, a):
        return add("V", lambda q: q.tensor_copy(out[0], a[0]), [a], [out], vdur(out[3]))

    def mset(out, v):
        f = 0.5 if SCRATCH[out[1]][2] in ("bfloat16", "uint16") else 1.0
        return add("V", lambda q: q.memset(out[0], v), [], [out], vdur(out[3], f))

    def scan(out, d0, d1, op0, op1):
        return add("V", lambda q: q.tensor_tensor_scan(out[0], d0[0], d1[0], 0.0, op0, op1), [d0, d1], [out], vdur(out[3]))

    def act(out, a, func, bias=None, extra=()):
        kw = {} if bias is None else {"bias": bias}
        return add("S", lambda q: q.activation(out[0], a[0], func, **kw), [a] + list(extra), [out], (65 + out[3]) * CYC)

    def mm(out, lst, start, stop):
        def e(q):
            for i, (l, r) in enumerate(lst):
                ins = q.matmul(out[0], l[0], r[0], start and i == 0, stop and i == len(lst) - 1)
            return ins
        d = sum(max(64, r[3]) * (4 if SCRATCH[r[1]][2] == "float32" else 1) for l, r in lst) * PEC
        return add("P", e, [x for p in lst for x in p], [out], d)

    def dma(eng, out, in_, sem, reads, writes, lat, order=()):
        return add(eng, lambda q: q.dma_start(out, in_), reads, writes, lat, sem=sem, cnt=16, lat=0, hold=60, order=order)

    sent = [0]

    def send(to, src, dst, sem, lat, after=(), order=()):
        c = T.cores[to % N]
        rid, pid, _ = topo.addr(c)
        ne = len(topo.engines(core, c))
        sent[0] += ne
        k = add("G", lambda q: q.remote_dma(dst[0], src[0], T.sem[sem], T.sem.left, pid, rid, topo.mask(core, c)),
                [src], [], ISSUE, sem="", after=after, order=order, lat=0)
        add(None, None, [], [dst], lat, sem=sem, cnt=ne, after=[k], lat=0)
        return k

    k = dma("Y", T.STI[:], T.st[:], "lst", [], [C("STI", 0, 32)], 2000)
    lf = dma("Y", T.F[:, 64:4160], T.fr[:, 0:4096], "lf", [], [C("F", 64, 4160)], LOAD - 200, [k])
    k = dma("S", T.Q[:, 0:512], T.qu[:], "lq", [], [C("Q", 0, 512)], 2300)
    lg = dma("S", T.F[:, 4160:8256], T.fr[:, 4096:8192], "lg", [], [C("F", 4160, 8256)], LOAD, [k])
    dma("S", T.JUI[:], T.ju[:], "lj", [], [C("JUI", 0, 64)], LOAD + 400, [lg])
    vcopy(C("F", 0, 64), C("F", 64, 128))
    vcopy(C("F", 8256, 8320), C("F", 8192, 8256))

    DD = C("DD", 0, 128)
    add("G", lambda q: q.iota(DD[0], [[1, 128]], 0, -1, allow_small_or_imprecise_dtypes=True), [], [DD], 350)
    add("G", lambda q: q.affine_select(DD[0], DD[0], [[-16, 8], [0, 16]], A.is_ge, 999.0, 0, 1), [DD], [DD], 400)
    add("G", lambda q: q.affine_select(DD[0], DD[0], [[16, 8], [0, 16]], A.is_ge, 999.0, 15, -1), [DD], [DD], 400)
    PI0, PI1 = C("PI", 0, 1), C("PI", 1, 2)
    add("G", lambda q: q.iota(PI0[0], [[0, 1]], 0, 1), [], [PI0], 140)
    ts(PI1, PI0, 15, None, A.bitwise_and)
    MK = (C("MK", 0, 1), C("MK", 1, 2))
    for t in (0, 1):
        ts(MK[t], PI1, 15.0 * t, BIG, A.is_equal, A.mult)
        ts(MK[t], MK[t], KS * FRAC[t][1] / 64, None, A.add)
    cf = lambda i: C("CF", 128 * i, 128 * i + 128)
    cb = lambda i: C("CB", 128 * i, 128 * i + 128)
    for i, v in enumerate((1.0, -15.0, -1.0, 15.0, 0.0)):
        ts(cf(i), DD, v, None, A.is_equal)
        ts(cb(i), DD, v, (1 / 64, 1 / 64, -1 / 64, -1 / 64, 1.0)[i], A.is_equal, A.mult)
    ts(cb(5), DD, 0.0, -2.0, A.is_equal, A.mult)
    mset(C("W", 0, 2048), 0.0)
    EB = C("EB", 0, 8)
    ts(EB, C("DD", 0, 128, 16), 999.0, KS, A.not_equal, A.mult)
    for r in range(16):
        act(C("W", 128 * r + r, 128 * r + 128, 16), EB, AF.Copy)
    Wr = lambda r: C("W", 128 * r, 128 * r + 128)
    mset(C("RST", 0, 384), 0.0)
    for t in (0, 1):
        ns, b = NS[t], 192 * t
        edge = C("KI", b + POS[t][1] + (0, 3)[t] * ns, b + 32 * ns, 4 * ns)
        for c in range(ns):
            mset(C("KI", b + POS[t][c], b + 32 * ns, ns), KS * FRAC[t][c] / 64 if c < 4 else KS * 16000)
        ts(edge, edge, 0.0, MK[t][0], A.mult, A.add, extra=[MK[t]])
        mset(C("KI", b + 2 + (0, 28)[t] * ns, b + (4, 32)[t] * ns, ns), BIG + KS * FRAC[t][2] / 64)
        mset(C("RST", b, b + 32 * ns, ns), 2.0 ** 30)
    mset(C("LAND", 0, LW), 128.0)
    for s in range(3):
        mset(C("MSG", s * LW, s * LW + 12), 128.0)
    for s in range(4):
        mset(C("SC", 384 * s + 128, 384 * s + 144), 128.0)
        mset(C("PA", 384 * s + 192 + POS[1][5], 384 * s + 384, NS[1]), 128.0)
        mset(C("L0", 72 * s + 68, 72 * s + 72), 0)
    ts(C("LAND", 12, LW, 3), C("STI", 0, 32), 1 / 64, 128.0, A.mult, A.add)
    ts(C("JF", 0, 64), C("JUI", 0, 64), 1 / 64, 128.0, A.mult, A.subtract)

    act(C("QSQ", 0, 512), C("Q", 0, 512), AF.Square)
    mm(C("KA0", 448, 480), [(Wr(r), C("QSQ", r, 512, 16)) for r in range(16)], True, True)
    act(C("Q2", 0, 32), C("KA0", 448, 480), AF.Copy)

    first = send(rank + 1, C("Q", 0, 512), C("Q", 512, 1024), "q1", 4500, after=[lf, lg])
    peers = [T.cores[(rank + j) % N] for j in (1, 2, 3)]
    m = topo.mask(core, peers[0]) & topo.mask(core, peers[1]) & topo.mask(core, peers[2])
    ne = bin(m).count("1")
    sent[0] += ne
    tr = RemoteDMATransfer(dst_ids=[DstId(rid=topo.addr(c)[0], pnc=topo.addr(c)[1]) for c in peers], dma_engine_mask=m,
                           remote_sem=T.sem.sq, srcs=[T.Q2[:, 0:32]], dsts=[T.Q2[:, 32 * j:32 * j + 32] for j in (1, 2, 3)])
    k = add("G", lambda q: q.remote_dma_fused([tr], local_sem=T.sem.left), [C("Q2", 0, 32)], [], ISSUE, sem="", order=[first], lat=0)
    add(None, None, [], [C("Q2", 32, 128)], 4000, sem="sq", cnt=3 * ne, after=[k], lat=0)

    for s in range(1, N):
        act(C("KI", 384 * s, 384 * s + 128), C("KI", 0, 128), AF.Copy)
        act(C("KI", 384 * s + 192, 384 * s + 384), C("KI", 192, 384), AF.Copy)
    for s in range(N):
        for (t, c) in SGATHER:
            ns, o = NS[t], 384 * s + 192 * t + POS[t][c]
            a, b = ((4, 32), (0, 28))[t] if c == 2 else (0, 32)
            act(C("KI", o + ns * a, o + ns * (b - 1) + 1, ns), C("Q2", 32 * s + a, 32 * s + b), AF.Identity, bias=KS * FRAC[t][c] / 64)
            if c == 1:
                a = (0, 3)[t]
                act(C("KI", o + ns * a, o + ns * 31 + 1, 4 * ns), C("Q2", 32 * s + a, 32 * s + 32, 4), AF.Identity,
                    bias=MK[t][0], extra=[MK[t]])

    WIN = {0: 64, 1: 128, -1: 0}

    def star(s, t, a, b):
        if t == 0:
            o = s * LW + 12
            return C("LAND", o + 3 * a, o + 3 * (b - 1) + 1, 3)
        o = 384 * s + 3
        return C("SC", o + 4 * a, o + 4 * (b - 1) + 1, 4)

    def lists0(s, t, a, b):
        o = 72 * s + (4, 36)[t]
        ts(C("L0", o + a, o + b), star(s, t, a, b), 64.0, 8192.0, A.mult, A.subtract)

    def sweep(s, t, x):
        c0, c1 = 4 * CUTS[s][x], 4 * CUTS[s][x + 1]
        n, ns, u, sg = c1 - c0, NS[t], 2 * s + t, (1, -1)[t]
        slot = lambda nm, c: C(nm, 192 * u + ns * c0 + POS[t][c], 192 * u + ns * c1, ns)
        full = lambda nm, base: C(nm, base + ns * c0, base + ns * c1)
        SQ, nq = "SQ%d" % t, 4 - t
        kb = ("KA%d", "KB%d")[t] % x
        K, KQ, E, P1 = C(kb, 0, ns * n), C(kb, 0, ns * n, 1 + t), C(kb, 200, 200 + ns * n), C(kb, 400, 400 + n)
        me = star(s, t, c0, c1)
        if t == 1:
            lists0(s, 1, c0, c1)
        l0 = 72 * s + (4, 36)[t]
        a, b = (c0 - 1, c1) if t == 0 else (c0, c1 + 1)
        fo = (u * 3 + x) * 34
        YR, FL = C("YR", fo, fo + n + 1), C("FL", fo, fo + n + 1)
        if t == 0:
            act(YR, star(s, t, a, b), AF.Identity, bias=-61.0 / 128)
            tt(FL, YR, star(s, t, a, b), A.is_le)
            f_me, f_nb = C("FL", fo + 1, fo + n + 1), C("FL", fo, fo + n)
        else:
            act(YR, star(s, t, a, b), AF.Copy)
            tt(FL, YR, star(s, t, a, b), A.not_equal)
            f_me, f_nb = C("FL", fo, fo + n), C("FL", fo + 1, fo + n + 1)
        mm(P1, [(cf(2 * t), me), (cf(2 * t + 1), star(s, t, c0 - sg, c1 - sg))], True, False)
        mm(P1, [(cb(2 * t), f_me), (cb(2 * t + 1), f_nb)], False, True)
        ts(C("L1", 32 * u + c0, 32 * u + c1), P1, 64.0, 8192.0, A.mult, A.subtract)
        act(slot("PA", 1), P1, AF.Copy)
        S3, L3 = C("S3", 32 * u + c0, 32 * u + c1), C("L3", 32 * u + c0, 32 * u + c1)
        tt(S3, me, C("JF", 32 * t + c0, 32 * t + c1), A.add)
        ts(L3, S3, 128 - 1 / 64, 64.0, A.min, A.mult)
        ts(slot("PA", 3), L3, 1 / 64, 128.0, A.mult, A.add)
        LT, nb = C("LT", 32 * u + c0, 32 * u + c1), star(s, t, c0 - 4 * sg, c1 - 4 * sg)
        ts(LT, nb, (255.0, 129.0)[t], None, (A.is_lt, A.is_ge)[t])
        tt(slot("PA", 2), nb, LT, (A.add, A.subtract)[t])
        act(slot("PA", 0), me, AF.Copy)
        if t == 1:
            act(slot("KI", 0), C("MM", 384 * s + 4 * c0 + 3, 384 * s + 4 * c1, 4), AF.Copy)
            o = s * LW + 12
            act(slot("PA", 4), C("LAND", o + 3 * c0 + 1, o + 3 * c1, 3), AF.Copy)
            if s > 0:
                act(slot("KI", 4), C("LAND", o + 3 * c0 + 2, o + 3 * c1, 3), AF.Copy)
        offs = {0: ("L0", l0), 1: ("L1", 32 * u), 2: ("L0", l0 - 4 * sg), 3: ("L3", 32 * u)}
        qq = C("Q", 512 * s + 16 * c0, 512 * s + 16 * c1)
        nd = 0
        for c in ((0, 2, 3, 1) if t == 0 else (2, 3, 1)):
            w0 = WIN[sg if c == 2 else 0]
            win = C("F", w0, w0 + 8192)
            of = C(offs[c][0], offs[c][1] + c0, offs[c][1] + c1)
            df = C("DF", 512 * (4 * t + c) + 16 * c0, 512 * (4 * t + c) + 16 * c1)
            sq = R(SQ, slice(nq * c0 + c - t, nq * c1, nq), slice(None))
            if (t, c) in SGATHER:
                D = C("DP%d_%d" % (x, nd % ND), 0, 16 * n)
                nd += 1
                mm(D, [(cb(5), qq)], True, False)
                add("S", lambda q, df=df, win=win, of=of: q.activation(df[0], win[0].indirect(of[0]), AF.Copy),
                    [win, of], [df], (65 + df[3] * GAM) * CYC)
                mm(D, [(cb(4), df)], False, True)
                tt(sq, D, df, A.mult)
            else:
                add("V", lambda q, df=df, win=win, of=of: q.tensor_tensor(df[0], win[0].indirect(of[0]), qq[0], A.subtract),
                    [win, of, qq], [df], (50 + df[3] * GAM) * CYC)
                act(sq, df, AF.Square)
        mm(K, [(cf(4), full("KI", 192 * u))], True, False)
        mm(KQ, [(Wr(r), R(SQ, slice(nq * c0, nq * c1), r)) for r in range(16)], False, True)
        M = full("MM", 192 * u)
        scan(M, C("RST", 192 * t, 192 * t + ns * n), K, A.add, A.min)
        tt(E, K, M, A.subtract)
        tt(full("BV", 192 * t), full("PA", 192 * u), E, A.subtract)
        scan(full("SC", 192 * u), E, full("BV", 192 * t), A.min, A.max)
        if t == 0:
            return None
        if s < 3:
            o = s * LW + 12
            act(C("MSG", o + 3 * c0 + 2, o + 3 * c1, 3), slot("MM", 4), AF.Identity, bias=-KS / 4)
            vcopy(C("MSG", o + 3 * c0, o + 3 * c1, 3), slot("SC", 3))
            act(C("MSG", o + 3 * c0 + 1, o + 3 * c1, 3), slot("SC", 4), AF.Copy)
            a = c0 if c0 else -4
            k = send(rank + 1, C("MSG", o + 3 * a, o + 3 * c1), C("LAND", o + LW + 3 * a, o + LW + 3 * c1), "a%d_%d" % (s + 1, x), HOP)
            lists0(s + 1, 0, a, c1)
            return k
        owner = (rank + 1) % N
        best = slot("MM", 4)
        ci, fi = C("AI", 2 * c0, 2 * c0 + n), C("AI", 2 * c0 + n, 2 * c1)
        ts(ci, best, 1 / KS, 0.33, A.mult, A.add)
        ts(fi, best, 4 / KS, owner + 3 - 0.19, A.mult, A.add)
        ts(fi, fi, 3, None, A.bitwise_and)
        vcopy(C("FMSG", 3 * c0 + n, 3 * c1), C("AI", 2 * c0, 2 * c1))
        ts(C("FMSG", 3 * c0, 3 * c0 + n), slot("SC", 4), 128.0, 64.0, A.subtract, A.mult)
        k = send(rank + 1, C("FMSG", 3 * c0, 3 * c1), C("FLAND", 3 * c0, 3 * c1), "a4_%d" % x, HOP)
        for j, y in enumerate((T.yp, T.yc, T.yf)):
            src = C("FLAND", 3 * c0 + j * n, 3 * c0 + (j + 1) * n)
            dma("S" if (x == 0 and j == 1) else "Y", y[:, c0:c1], src[0], "o%d_%d" % (x, j), [src], [], 2000)
        return k

    lists0(0, 0, -4, 32)
    for s in range(N):
        xs = list(range(NSTR - 1, -1, -1))
        for x in xs:
            sweep(s, 0, x)
        for x in xs:
            last = sweep(s, 1, x)
        if s < 2:
            send(rank + s + 2, C("Q", 0, 512), C("Q", 512 * (s + 2), 512 * (s + 3)), "q%d" % (s + 2), 4000, order=[last])
    return ops, sent[0]


def links(ops):
    return [[(j, ops[j]["dur"] + ops[j]["lat"]) for j in sorted(o["deps"])] + [(j, ops[j]["hold"]) for j in sorted(o["soft"])] for o in ops]


def schedule(ops):
    n, pre = len(ops), links(ops)
    succ = [[] for _ in ops]
    for k in range(n):
        for j, d in pre[k]:
            succ[j].append((k, d))
    prio = [0.0] * n
    for k in range(n - 1, -1, -1):
        prio[k] = ops[k]["dur"] + ops[k]["lat"] + max([prio[j] for j, _ in succ[k]] or [0.0])
    left, ready, free, order = [len(p) for p in pre], [0.0] * n, {}, []
    avail = [k for k in range(n) if left[k] == 0]
    while avail:
        k = min(avail, key=lambda k: (max(ready[k], free.get(ops[k]["eng"], 0.0)), -prio[k], k))
        avail.remove(k)
        st = max(ready[k], free.get(ops[k]["eng"], 0.0))
        if ops[k]["eng"]:
            free[ops[k]["eng"]] = st + ops[k]["hold"]
        order.append(k)
        for j, d in succ[k]:
            ready[j] = max(ready[j], st + d)
            left[j] -= 1
            if left[j] == 0:
                avail.append(j)
    return order


def replay(p, order):
    eng, dur, hold, pre = p
    free, last, st, why, end, ek = {}, {}, [0.0] * len(eng), [None] * len(eng), 0.0, 0
    for k in order:
        e = eng[k]
        t, w = free.get(e, 0.0), (last.get(e), 1)
        for j, d in pre[k]:
            if st[j] + d > t:
                t, w = st[j] + d, (j, 0)
        st[k], why[k] = t, w
        if e:
            free[e], last[e] = t + hold[k], k
        if t + dur[k] > end:
            end, ek = t + dur[k], k
    return end, ek, why


def improve(sets, order):
    ps = [([o["eng"] for o in s], [o["dur"] for o in s], [o["hold"] for o in s], links(s)) for s in sets]
    eng, pre = ps[0][0], ps[0][3]
    seed = [12345]

    def rnd():
        seed[0] = (seed[0] * 6364136223846793005 + 1442695040888963407) % (1 << 64)
        return (seed[0] >> 11) / float(1 << 53)

    res = [replay(p, order) for p in ps]
    unit = [r[0] for r in res]
    cur = float(len(ps))
    best = (cur, order)
    for it in range(ROUNDS):
        r = res[int(rnd() * len(res))]
        k, q = r[1], []
        while k is not None:
            j, queued = r[2][k]
            if queued and j is not None:
                q.append((j, k))
            k = j
        b, k = q[int(rnd() * len(q))]
        pos = {v: i for i, v in enumerate(order)}
        i = pos[b]
        for _ in range(int(rnd() * 4) if rnd() < 0.5 else 0):
            i -= 1
            while i >= 0 and eng[order[i]] != eng[k]:
                i -= 1
            if i >= 0:
                b = order[i]
        anc, stack = {k}, [k]
        while stack:
            for j, _ in pre[stack.pop()]:
                if pos[j] >= pos[b] and j not in anc:
                    anc.add(j)
                    stack.append(j)
        if b in anc:
            continue
        seg = order[pos[b]:pos[k] + 1]
        new = order[:pos[b]] + [v for v in seg if v in anc] + [v for v in seg if v not in anc] + order[pos[k] + 1:]
        res2 = [replay(p, new) for p in ps]
        c = sum(x[0] / w for x, w in zip(res2, unit))
        if c <= cur or rnd() < math.exp((cur - c) / (0.003 * (1 - it / ROUNDS) + 1e-5)):
            cur, res, order = c, res2, new
            if c < best[0]:
                best = (c, new)
    return best[1]


def rank_program(g, core, T, topo):
    if T.rank_of(core) is None:
        return
    ops, sent = build(g, core, T, topo, PARS[0])
    if not _ORDER:
        _ORDER.extend(improve([build(g, core, T, topo, p)[0] for p in PARS], schedule(ops)))
    order = _ORDER
    place = {k: i for i, k in enumerate(order)}
    queue = {"V": g.vector, "S": g.scalar, "P": g.tensor, "G": g, "Y": g.sync}
    count = {e: 0 for e in "VSPG"}
    known = {e: {} for e in queue}
    token, clock = {}, {}
    for k in order:
        o = ops[k]
        e = o["eng"]
        if e is None:
            token[k], clock[k] = (o["sem"], o["cnt"]), {}
            continue
        kn, need = known[e], {}
        for j in o["deps"]:
            sem, val = token[j]
            need[sem] = max(need.get(sem, (0, 0)), (val, j))
        for sem, (val, j) in sorted(need.items(), key=lambda it: -place[it[1][1]]):
            if kn.get(sem, 0) >= val:
                continue
            queue[e].wait_ge(T.sem[sem], val)
            kn[sem] = val
            for s2, v2 in clock[j].items():
                kn[s2] = max(kn.get(s2, 0), v2)
        ins = o["emit"](queue[e])
        clock[k] = dict(kn)
        if o["sem"] is None:
            count[e] += 1
            ins.then_inc(T.sem["c" + e], 1)
            token[k] = ("c" + e, count[e])
        elif o["sem"]:
            ins.then_inc(T.sem[o["sem"]], 16)
            token[k] = (o["sem"], 16)
    top = {"left": sent}
    for sem, val in token.values():
        top[sem] = max(top.get(sem, 0), val)
    anyq = {}
    for kn in known.values():
        for sem, val in kn.items():
            anyq[sem] = max(anyq.get(sem, 0), val)
    for sem, val in top.items():
        if anyq.get(sem, 0) < val:
            g.wait_ge(T.sem[sem], val)
